import numpy as np
import ml_dtypes


def mxq(x, axis, fmt="e4m3"):
    dtype, down = {"e4m3": (ml_dtypes.float8_e4m3fn, 7), "e5m2": (ml_dtypes.float8_e5m2, 14)}[fmt]
    v = np.moveaxis(np.asarray(x, np.float32).astype(ml_dtypes.bfloat16).astype(np.float64), axis, -1)
    blocks = v.reshape(v.shape[:-1] + (-1, 32))
    amax = np.abs(blocks).max(-1, keepdims=True)
    byte = np.maximum(np.where(amax > 0, np.frexp(amax)[1] - 1 + 127, 0) - down, 1)
    scale = np.exp2(byte - 127.0)
    codes = (blocks / scale).astype(np.float32).astype(dtype).astype(np.float64)
    return np.moveaxis((codes * scale).reshape(v.shape), -1, axis)


WIDE = False


def mx_kscale(k):
    if not WIDE:
        return np.ones(k)
    levels = np.array([10, -10, 5, -5, 0])
    if k % 512:
        return np.exp2(np.random.permutation(np.resize(levels, k // 32))).repeat(32)
    a = np.empty((k // 512, 16))
    for p in range(k // 512):
        a[p, :8] = np.random.permutation(np.resize(levels, 8))
        for g in range(8):
            far = levels[np.abs(levels - a[p, g]) >= 10]
            a[p, g + 8] = far[np.random.randint(len(far))]
    return np.exp2(a.ravel()).repeat(32)


def f64(x):
    return np.asarray(x).astype(np.float64)


def striped(idx):
    return np.tile(idx.reshape(-1, 16).T, (8, 1)).astype(np.uint16)


def unstriped(offs):
    return offs[:16].T.reshape(-1).astype(np.int64)


def striped8(idx):
    return np.concatenate([x.reshape(-1, 16).T for x in idx]).astype(np.uint16)


def runs(offs, k):
    lists = np.stack([offs[16 * r : 16 * r + 16].T.reshape(-1) for r in range(8)]).astype(np.int64)
    return lists[np.arange(k) % 512 // 64]


def pack_weight(w):
    k, n = w.shape
    w = f64(np.asarray(w, np.float32).astype(ml_dtypes.bfloat16)).reshape(k // 32, 32, n)
    amax = np.abs(w).max(1)
    byte = np.clip(np.where(amax > 0, np.frexp(amax)[1] - 1 + 127 - 7, 1), 1, 254)
    scaled = (w * np.exp2(127.0 - byte)[:, None, :]).reshape(k, n).astype(np.float32)
    words = np.ascontiguousarray(scaled.reshape(k // 512, 128, 4, n).transpose(0, 1, 3, 2)).astype(ml_dtypes.float8_e4m3fn).view(np.uint8)
    return words, np.ascontiguousarray(byte.astype(np.uint8).reshape(k // 512, 16, n))


def unpack_weight(words, scales):
    g, p, n, _ = words.shape
    vals = np.ascontiguousarray(words).view(ml_dtypes.float8_e4m3fn).astype(np.float64) * np.repeat(np.exp2(scales.astype(np.float64) - 127.0), 8, axis=1)[..., None]
    return vals.transpose(0, 1, 3, 2).reshape(g * 512, n)


K, T, S, H, W = 512, 2048, 512, 512, 256


def setup_inputs():
    n = np.random.standard_normal
    s = mx_kscale(K)[:, None]
    u = mx_kscale(S)
    packed_xT = pack_weight(n((K, T)) * s)
    perm = np.stack([np.random.permutation(S) for _ in range(8)])
    return {
        "x_words": packed_xT[0],
        "x_scales": packed_xT[1],
        "w1": (n((K, H)) / np.sqrt(K) / s).astype(np.float32),
        "ga": (np.random.uniform(0.5, 1.5, (H, 1)) * u[:, None]).astype(np.float32),
        "gb": (np.random.uniform(0.5, 1.5, (H, 1)) / u[:, None]).astype(np.float32),
        "offs": striped(np.random.permutation(T)[:S]),
        "n1": striped8(np.stack([np.random.permutation(S) for _ in range(8)])),
        "n2": striped8(np.stack([np.random.permutation(S) for _ in range(8)])),
        "n3": striped8(np.stack([np.random.permutation(S) for _ in range(8)])),
        "n4": striped8(perm[:, :W]),
        "n5": striped8(perm[:, W:]),
    }


def reference(x_words, x_scales, w1, ga, gb, offs, n1, n2, n3, n4, n5):
    xq = unpack_weight(x_words, x_scales)[:, unstriped(offs)]
    y = mxq(f64(w1), 0, "e4m3").T @ xq
    z = f64(ga) * (y / (np.abs(y[np.arange(H)[:, None], runs(n1, H)]) + 0.5))
    st = y - (y[np.arange(H)[:, None], runs(n2, H)])
    z2 = f64(gb) * (st / (np.abs(st[np.arange(H)[:, None], runs(n3, H)]) + 0.5))
    s = 0.0625 * ((mxq(z, 0, "e4m3").T @ mxq(z2, 0, "e4m3")))
    pb = s[np.arange(S)[:, None], runs(n5, S)]
    pa = s[np.arange(S)[:, None], runs(n4, S)]
    rb = pb - (0.5 * pa)
    ra = np.sqrt((pa) ** 2 + (pb) ** 2 + 0.25)
    ds = np.zeros((S, S))
    ds[np.arange(S)[:, None], runs(n4, S)] = ra
    out = ds.copy()
    out[np.arange(S)[:, None], runs(n5, S)] = rb
    return out

@@ -1,0 +1,252 @@
+from contextlib import ExitStack
+
+import concourse.mybir as mybir
+
+K, T, S, H, W = 512, 2048, 512, 512, 256
+FLOPS = 2 * K * H * S + 2 * H * S * S
+
+F32 = mybir.dt.float32
+BF16 = mybir.dt.bfloat16
+I32 = mybir.dt.int32
+U32 = mybir.dt.uint32
+U16 = mybir.dt.uint16
+U8 = mybir.dt.uint8
+FP8X4 = mybir.dt.float8_e4m3fn_x4
+ACT = mybir.ActivationFunctionType
+ALU = mybir.AluOpType
+
+P = 128
+PACK = 4
+VECTOR_FETCHED = 2
+CHUNKS = [(0, 256), (256, 384), (384, 512)]
+W_SPLIT = 44
+
+
+def tile_picked_selfnormhopnpolar_none_p_kernel(
+    tc, x_words, x_scales, w1, ga, gb, offs, n1, n2, n3, n4, n5, out
+):
+    nc = tc.nc
+    with ExitStack() as ctx:
+        keep = ctx.enter_context(tc.tile_pool(name="keep", bufs=1))
+        psum = ctx.enter_context(tc.psum_pool(name="psum", bufs=1))
+
+        def load_list(src, name):
+            t = keep.tile([P, src.shape[1]], U16, name=name)
+            nc.sync.dma_start(t[:], src)
+            return t
+
+        x_bytes = keep.tile([P, T], U8, name="x_bytes", align_bytes=64)
+        nc.gpsimd.memset(x_bytes[:].bitcast(I32), 0)
+        for q in range(4):
+            nc.scalar.dma_start(x_bytes[32 * q : 32 * q + 4, :].bitcast(I32), x_scales[0, 4 * q : 4 * q + 4, :].bitcast(I32))
+
+        offs_sb = load_list(offs, "offs_sb")
+        x_table = keep.tile([P, T], I32, name="x_table", align_bytes=64)
+        nc.sync.dma_start(x_table[:], x_words[0].rearrange("p n t -> p (n t)").bitcast(I32))
+        w_rows = w1.rearrange("(p j) c -> p j c", j=PACK)
+        w_raw = [keep.tile([P, PACK, H // 2], F32, name=f"w_raw{h}") for h in range(2)]
+        for h in range(2):
+            nc.sync.dma_start(w_raw[h][:], w_rows[:, :, h * (H // 2) : (h + 1) * (H // 2)])
+        n2_sb = load_list(n2, "n2_sb")
+        n1_sb = load_list(n1, "n1_sb")
+        n3_sb = load_list(n3, "n3_sb")
+        n4_sb = load_list(n4, "n4_sb")
+        n5_sb = load_list(n5, "n5_sb")
+        ga_sb = keep.tile([P, PACK], F32, name="ga_sb")
+        nc.sync.dma_start(ga_sb[:], ga.rearrange("(p t) o -> p (t o)", t=PACK))
+        gb_sb = keep.tile([P, PACK], F32, name="gb_sb")
+        nc.sync.dma_start(gb_sb[:], gb.rearrange("(p t) o -> p (t o)", t=PACK))
+
+        y_win = [keep.tile([P, 2 * S], F32, name=f"y_win{t}") for t in range(PACK)]
+        nc.gpsimd.memset(y_win[0][:, S:], 0.0)
+        half = keep.tile([P, 1], F32, name="half")
+        nc.gpsimd.memset(half[:], 0.5)
+        quarter = keep.tile([P, 1], F32, name="quarter")
+        nc.gpsimd.memset(quarter[:], 0.25)
+        warm = keep.tile([P, 1], F32, name="warm")
+        nc.scalar.activation(warm[:], half[:], ACT.Ln, bias=half[:])
+        for t in range(1, PACK):
+            nc.vector.memset(y_win[t][:, S:], 0.0)
+
+        xw = keep.tile([P, S], U32, name="xw", align_bytes=64)
+        nc.vector.tensor_copy(xw[:], x_table[:].bitcast(U32).indirect(offs_sb[:]))
+        xs = keep.tile([P, S], U8, name="xs", align_bytes=64)
+        nc.vector.tensor_copy(xs[:], x_bytes[:].indirect(offs_sb[:]))
+
+        w_bf = keep.tile([P, PACK * H], BF16, name="w_bf", align_bytes=64)
+        w_dst = w_bf[:].rearrange("p (t m j) -> p m j t", t=PACK, j=PACK)
+        w_src = [w_raw[h][:].rearrange("p j (m t) -> p m j t", t=PACK) for h in range(2)]
+        nc.scalar.copy(w_dst[:, :64], w_src[0])
+        nc.vector.tensor_copy(w_dst[:, 64 : 64 + W_SPLIT], w_src[1][:, :W_SPLIT])
+        nc.scalar.copy(w_dst[:, 64 + W_SPLIT :], w_src[1][:, W_SPLIT:])
+        w_codes = keep.tile([P, H], U32, name="w_codes", align_bytes=64)
+        w_scales = keep.tile([P, H], U8, name="w_scales", align_bytes=64)
+        for t in range(PACK):
+            cols = slice(t * P, (t + 1) * P)
+            nc.vector.quantize_mx(
+                out=w_codes[:, cols].bitcast(FP8X4), scales=w_scales[:, cols], in_=w_bf[:, t * H : (t + 1) * H]
+            )
+
+        y_ps = [psum.tile([P, S], F32, name=f"y_ps{t}") for t in range(PACK)]
+        for t in range(PACK):
+            cols = slice(t * P, (t + 1) * P)
+            nc.tensor.matmul_mx(
+                out=y_ps[t][:], lhsT=w_codes[:, cols].bitcast(FP8X4), lhsT_scale=w_scales[:, cols],
+                rhs=xw[:].bitcast(FP8X4), rhs_scale=xs[:], start=True, stop=True,
+            )
+
+        recip = keep.tile([P, 2 * PACK, S], F32, name="recip")
+        log1 = [keep.tile([P, 2 * S], F32, name=f"log1_{t}") for t in range(PACK)]
+        log2 = [keep.tile([P, S], F32, name=f"log2_{t}") for t in range(PACK)]
+        hop = [keep.tile([P, S], F32, name=f"hop{t}", tag=f"hop{t}") for t in range(PACK)]
+        st = keep.tile([P, PACK, S], F32, name="st")
+        mag = [keep.tile([P, S], F32, name=f"mag{t}") for t in range(PACK - 1)]
+        runs = lambda ap: ap.rearrange("p (a b) -> p a b", b=16)
+        last_mag = recip[:].rearrange("p r (a b) -> p (r a) b", b=P)[:, :, 0:16]
+
+        def mag_of(t):
+            return last_mag if t == PACK - 1 else runs(mag[t][:])
+
+        def evac(t):
+            nc.scalar.copy(y_win[t][:, :S], y_ps[t][:])
+
+        def abs_y(t):
+            nc.scalar.activation(log1[t][:, S:], y_ps[t][:], ACT.Abs)
+
+        def log_y(t):
+            nc.scalar.activation(log1[t][:, :S], log1[t][:, S:], ACT.Ln, bias=half[:])
+
+        def fetch_hop(t):
+            nc.vector.tensor_copy(hop[t][:], y_win[t][:].indirect(n2_sb[:]))
+
+        def step(t):
+            nc.vector.tensor_tensor(st[:, t, :], y_win[t][:, :S], hop[t][:], ALU.subtract)
+
+        def abs_st_vector(t):
+            nc.vector.scalar_tensor_tensor(mag_of(t), runs(st[:, t, :]), -1.0, runs(st[:, t, :]), ALU.mult, ALU.max)
+
+        def abs_st_scalar(t):
+            nc.scalar.activation(mag_of(t), runs(st[:, t, :]), ACT.Abs)
+
+        def log_st(t):
+            nc.scalar.activation(runs(log2[t][:]), mag_of(t), ACT.Ln, bias=half[:])
+
+        for t in range(PACK):
+            evac(t)
+        fetch_hop(0)
+        fetch_hop(1)
+        abs_y(0)
+        abs_y(1)
+        step(0)
+        step(1)
+        log_y(0)
+        log_y(1)
+        abs_st_vector(0)
+        fetch_hop(2)
+        abs_st_vector(1)
+        fetch_hop(3)
+        abs_y(2)
+        abs_y(3)
+        log_st(0)
+        log_y(2)
+        log_st(1)
+        log_y(3)
+        step(2)
+        step(3)
+        abs_st_scalar(2)
+        abs_st_vector(3)
+        log_st(2)
+        log_st(3)
+
+        late = keep.tile([P, 2 * PACK + VECTOR_FETCHED, S], F32, name="late", tag=f"hop{PACK - 1}")
+        ya = late[:, :PACK, :]
+        sb = late[:, PACK : 2 * PACK, :]
+        fetched = [late[:, 2 * PACK + t, :] for t in range(VECTOR_FETCHED)]
+        for t in range(VECTOR_FETCHED):
+            nc.vector.tensor_copy(fetched[t], log1[t][:].indirect(n1_sb[:]))
+        for t in range(PACK):
+            nc.vector.tensor_scalar_mul(ya[:, t, :], y_win[t][:, :S], ga_sb[:, t : t + 1])
+        for t in range(PACK):
+            nc.vector.tensor_scalar_mul(sb[:, t, :], st[:, t, :], gb_sb[:, t : t + 1])
+
+        for t in range(PACK):
+            src = fetched[t] if t < VECTOR_FETCHED else log1[t][:].indirect(n1_sb[:])
+            nc.scalar.activation(recip[:, t, :], src, ACT.Exp, scale=-1.0)
+
+        z_bf = keep.tile([P, PACK * S], BF16, name="z_bf", align_bytes=64)
+        dealt = "p t (m u) -> p m t u"
+        nc.vector.tensor_tensor(
+            z_bf[:].rearrange("p (u m t) -> p m t u", u=PACK, t=PACK),
+            ya.rearrange(dealt, u=PACK), recip[:, :PACK, :].rearrange(dealt, u=PACK), ALU.mult,
+        )
+        z_codes = keep.tile([P, S], U32, name="z_codes", align_bytes=64)
+        z_scales = keep.tile([P, S], U8, name="z_scales", align_bytes=64)
+        nc.vector.quantize_mx(out=z_codes[:].bitcast(FP8X4), scales=z_scales[:], in_=z_bf[:])
+
+        z2_bf = keep.tile([P, PACK * S], BF16, name="z2_bf", align_bytes=64)
+        z2_codes = keep.tile([P, S], U32, name="z2_codes", align_bytes=64)
+        z2_scales = keep.tile([P, S], U8, name="z2_scales", align_bytes=64)
+        woven = "p t (c i) -> p c t i"
+        for a, b in CHUNKS:
+            for t in range(PACK):
+                nc.scalar.activation(
+                    recip[:, PACK + t, a:b], log2[t][:].indirect(n3_sb[:, a // 16 : b // 16]), ACT.Exp, scale=-1.0
+                )
+            nc.vector.tensor_tensor(
+                z2_bf[:, PACK * a : PACK * b].rearrange("p (c i t) -> p c t i", i=4, t=PACK),
+                sb[:, :, a:b].rearrange(woven, i=4), recip[:, PACK:, a:b].rearrange(woven, i=4), ALU.mult,
+            )
+            nc.vector.quantize_mx(
+                out=z2_codes[:, a:b].bitcast(FP8X4), scales=z2_scales[:, a:b], in_=z2_bf[:, PACK * a : PACK * b]
+            )
+
+        s_win = [keep.tile([P, S], F32, name=f"s_win{u}") for u in range(PACK)]
+
+        def product(u, pieces, bank):
+            cols = slice(u * P, (u + 1) * P)
+            for a, b in pieces:
+                nc.tensor.matmul_mx(
+                    out=bank[:, a:b], lhsT=z_codes[:, cols].bitcast(FP8X4), lhsT_scale=z_scales[:, cols],
+                    rhs=z2_codes[:, a:b].bitcast(FP8X4), rhs_scale=z2_scales[:, a:b], start=True, stop=True,
+                )
+            a, b = pieces[0][0], pieces[-1][1]
+            nc.scalar.activation(s_win[u][:, a:b], bank[:, a:b], ACT.Copy, scale=0.0625)
+
+        s_early = psum.tile([P, S], F32, name="y_ps0")
+        product(0, CHUNKS[:-1], s_early)
+        for u in range(PACK):
+            s_ps = psum.tile([P, S], F32, name=f"s_ps{u}")
+            product(u, CHUNKS[-1:] if u == 0 else [(0, S)], s_ps)
+
+        out_rows = out.rearrange("(m u) j -> u m j", u=PACK)
+        pa = [keep.tile([P, W], F32, name=f"pa{u}") for u in range(PACK)]
+        pb = [keep.tile([P, W], F32, name=f"pb{u}") for u in range(PACK)]
+        sq = [keep.tile([P, 2, W], F32, name=f"sq{u}") for u in range(PACK)]
+        ssum = [keep.tile([P, W], F32, name=f"ssum{u}") for u in range(PACK)]
+        ra = [keep.tile([P, W], F32, name=f"ra{u}") for u in range(PACK)]
+        res = [keep.tile([P, S], F32, name=f"res{u}") for u in range(PACK)]
+
+        def fetch(u):
+            nc.vector.tensor_scalar(pa[u][:], s_win[u][:].indirect(n4_sb[:]), -0.5, 0.0, ALU.mult, ALU.add)
+            nc.vector.tensor_copy(pb[u][:], s_win[u][:].indirect(n5_sb[:]))
+            nc.scalar.activation(sq[u][:, 0, :], pa[u][:], ACT.Square, scale=2.0)
+            nc.scalar.activation(sq[u][:, 1, :], pb[u][:], ACT.Square)
+
+        def put_rb(u):
+            nc.vector.tensor_tensor(res[u][:].indirect(n5_sb[:]), pb[u][:], pa[u][:], ALU.add)
+
+        def radius(u):
+            nc.vector.tensor_tensor(ssum[u][:], sq[u][:, 0, :], sq[u][:, 1, :], ALU.add)
+            nc.scalar.activation(ra[u][:], ssum[u][:], ACT.Sqrt, bias=quarter[:])
+
+        def put_ra(u):
+            nc.vector.tensor_copy(res[u][:].indirect(n4_sb[:]), ra[u][:])
+            nc.sync.dma_start(out_rows[u], res[u][:])
+
+        fetch(0)
+        for u in range(PACK):
+            if u + 1 < PACK:
+                fetch(u + 1)
+            radius(u)
+            put_rb(u)
+            put_ra(u)

@@ -17,7 +17,7 @@ ALU = mybir.AluOpType
 
 P = 128
 PACK = 4
-VECTOR_FETCHED = 2
+VECTOR_FETCHED = 4
 CHUNKS = [(0, 256), (256, 384), (384, 512)]
 W_SPLIT = 44
 
@@ -128,11 +128,21 @@ def tile_picked_selfnormhopnpolar_none_p_kernel(
         def abs_st_scalar(t):
             nc.scalar.activation(mag_of(t), runs(st[:, t, :]), ACT.Abs)
 
+        ya = keep.tile([P, PACK, S], F32, name="ya")
+        sb = keep.tile([P, PACK, S], F32, name="sb", tag="sb", align_bytes=64)
+
+        def gain_y(t):
+            nc.gpsimd.tensor_scalar(ya[:, t, :], y_win[t][:, :S], ga_sb[:, t : t + 1], 0.0, ALU.mult, ALU.add)
+
+        def gain_st(t):
+            nc.gpsimd.tensor_scalar(sb[:, t, :], st[:, t, :], gb_sb[:, t : t + 1], 0.0, ALU.mult, ALU.add)
+
         def log_st(t):
             nc.scalar.activation(runs(log2[t][:]), mag_of(t), ACT.Ln, bias=half[:])
 
         for t in range(PACK):
             evac(t)
+            gain_y(t)
         fetch_hop(0)
         fetch_hop(1)
         abs_y(0)
@@ -157,31 +167,24 @@ def tile_picked_selfnormhopnpolar_none_p_kernel(
         abs_st_vector(3)
         log_st(2)
         log_st(3)
+        for t in range(PACK):
+            gain_st(t)
 
-        late = keep.tile([P, 2 * PACK + VECTOR_FETCHED, S], F32, name="late", tag=f"hop{PACK - 1}")
-        ya = late[:, :PACK, :]
-        sb = late[:, PACK : 2 * PACK, :]
-        fetched = [late[:, 2 * PACK + t, :] for t in range(VECTOR_FETCHED)]
-        for t in range(VECTOR_FETCHED):
-            nc.vector.tensor_copy(fetched[t], log1[t][:].indirect(n1_sb[:]))
+        fetched = keep.tile([P, PACK, S], F32, name="fetched", tag=f"hop{PACK - 1}")
         for t in range(PACK):
-            nc.vector.tensor_scalar_mul(ya[:, t, :], y_win[t][:, :S], ga_sb[:, t : t + 1])
+            nc.vector.tensor_copy(fetched[:, t, :], log1[t][:].indirect(n1_sb[:]))
         for t in range(PACK):
-            nc.vector.tensor_scalar_mul(sb[:, t, :], st[:, t, :], gb_sb[:, t : t + 1])
-
-        for t in range(PACK):
-            src = fetched[t] if t < VECTOR_FETCHED else log1[t][:].indirect(n1_sb[:])
-            nc.scalar.activation(recip[:, t, :], src, ACT.Exp, scale=-1.0)
+            nc.scalar.activation(recip[:, t, :], fetched[:, t, :], ACT.Exp, scale=-1.0)
 
         z_bf = keep.tile([P, PACK * S], BF16, name="z_bf", align_bytes=64)
         dealt = "p t (m u) -> p m t u"
         nc.vector.tensor_tensor(
             z_bf[:].rearrange("p (u m t) -> p m t u", u=PACK, t=PACK),
-            ya.rearrange(dealt, u=PACK), recip[:, :PACK, :].rearrange(dealt, u=PACK), ALU.mult,
+            ya[:].rearrange(dealt, u=PACK), recip[:, :PACK, :].rearrange(dealt, u=PACK), ALU.mult,
         )
-        z_codes = keep.tile([P, S], U32, name="z_codes", align_bytes=64)
+        z_first = keep.tile([P, P], U32, name="z_first", align_bytes=64)
         z_scales = keep.tile([P, S], U8, name="z_scales", align_bytes=64)
-        nc.vector.quantize_mx(out=z_codes[:].bitcast(FP8X4), scales=z_scales[:], in_=z_bf[:])
+        nc.vector.quantize_mx(out=z_first[:].bitcast(FP8X4), scales=z_scales[:, :P], in_=z_bf[:, :S])
 
         z2_bf = keep.tile([P, PACK * S], BF16, name="z2_bf", align_bytes=64)
         z2_codes = keep.tile([P, S], U32, name="z2_codes", align_bytes=64)
@@ -200,13 +203,19 @@ def tile_picked_selfnormhopnpolar_none_p_kernel(
                 out=z2_codes[:, a:b].bitcast(FP8X4), scales=z2_scales[:, a:b], in_=z2_bf[:, PACK * a : PACK * b]
             )
 
+        z_rest = keep.tile([P, S - P], U32, name="z_rest", tag="sb", align_bytes=64)
+        for a, b in [(1, 2), (2, 4)]:
+            nc.vector.quantize_mx(
+                out=z_rest[:, (a - 1) * P : (b - 1) * P].bitcast(FP8X4), scales=z_scales[:, a * P : b * P], in_=z_bf[:, a * S : b * S]
+            )
+        z_codes = [z_first[:]] + [z_rest[:, u * P : (u + 1) * P] for u in range(PACK - 1)]
         s_win = [keep.tile([P, S], F32, name=f"s_win{u}") for u in range(PACK)]
 
         def product(u, pieces, bank):
             cols = slice(u * P, (u + 1) * P)
             for a, b in pieces:
                 nc.tensor.matmul_mx(
-                    out=bank[:, a:b], lhsT=z_codes[:, cols].bitcast(FP8X4), lhsT_scale=z_scales[:, cols],
+                    out=bank[:, a:b], lhsT=z_codes[u].bitcast(FP8X4), lhsT_scale=z_scales[:, cols],
                     rhs=z2_codes[:, a:b].bitcast(FP8X4), rhs_scale=z2_scales[:, a:b], start=True, stop=True,
                 )
             a, b = pieces[0][0], pieces[-1][1]
@@ -236,7 +245,7 @@ def tile_picked_selfnormhopnpolar_none_p_kernel(
             nc.vector.tensor_tensor(res[u][:].indirect(n5_sb[:]), pb[u][:], pa[u][:], ALU.add)
 
         def radius(u):
-            nc.vector.tensor_tensor(ssum[u][:], sq[u][:, 0, :], sq[u][:, 1, :], ALU.add)
+            nc.gpsimd.tensor_tensor(ssum[u][:], sq[u][:, 0, :], sq[u][:, 1, :], ALU.add)
             nc.scalar.activation(ra[u][:], ssum[u][:], ACT.Sqrt, bias=quarter[:])
 
         def put_ra(u):

@@ -19,7 +19,8 @@ P = 128
 PACK = 4
 VECTOR_FETCHED = 4
 CHUNKS = [(0, 256), (256, 384), (384, 512)]
-W_SPLIT = 44
+W_SPLIT = 40
+W_GPSIMD = 24
 
 
 def tile_picked_selfnormhopnpolar_none_p_kernel(
@@ -36,19 +37,20 @@ def tile_picked_selfnormhopnpolar_none_p_kernel(
             return t
 
         x_bytes = keep.tile([P, T], U8, name="x_bytes", align_bytes=64)
-        nc.gpsimd.memset(x_bytes[:].bitcast(I32), 0)
+        nc.gpsimd.memset(x_bytes[:, : T // 2].bitcast(I32), 0)
+        nc.vector.memset(x_bytes[:, T // 2 :].bitcast(I32), 0)
         for q in range(4):
             nc.scalar.dma_start(x_bytes[32 * q : 32 * q + 4, :].bitcast(I32), x_scales[0, 4 * q : 4 * q + 4, :].bitcast(I32))
 
         offs_sb = load_list(offs, "offs_sb")
+        n2_sb = load_list(n2, "n2_sb")
+        n1_sb = load_list(n1, "n1_sb")
         x_table = keep.tile([P, T], I32, name="x_table", align_bytes=64)
         nc.sync.dma_start(x_table[:], x_words[0].rearrange("p n t -> p (n t)").bitcast(I32))
         w_rows = w1.rearrange("(p j) c -> p j c", j=PACK)
         w_raw = [keep.tile([P, PACK, H // 2], F32, name=f"w_raw{h}") for h in range(2)]
         for h in range(2):
             nc.sync.dma_start(w_raw[h][:], w_rows[:, :, h * (H // 2) : (h + 1) * (H // 2)])
-        n2_sb = load_list(n2, "n2_sb")
-        n1_sb = load_list(n1, "n1_sb")
         n3_sb = load_list(n3, "n3_sb")
         n4_sb = load_list(n4, "n4_sb")
         n5_sb = load_list(n5, "n5_sb")
@@ -57,7 +59,7 @@ def tile_picked_selfnormhopnpolar_none_p_kernel(
         gb_sb = keep.tile([P, PACK], F32, name="gb_sb")
         nc.sync.dma_start(gb_sb[:], gb.rearrange("(p t) o -> p (t o)", t=PACK))
 
-        y_win = [keep.tile([P, 2 * S], F32, name=f"y_win{t}") for t in range(PACK)]
+        y_win = [keep.tile([P, (3 if t == PACK - 1 else 2) * S], F32, name=f"y_win{t}") for t in range(PACK)]
         nc.gpsimd.memset(y_win[0][:, S:], 0.0)
         half = keep.tile([P, 1], F32, name="half")
         nc.gpsimd.memset(half[:], 0.5)
@@ -76,7 +78,8 @@ def tile_picked_selfnormhopnpolar_none_p_kernel(
         w_bf = keep.tile([P, PACK * H], BF16, name="w_bf", align_bytes=64)
         w_dst = w_bf[:].rearrange("p (t m j) -> p m j t", t=PACK, j=PACK)
         w_src = [w_raw[h][:].rearrange("p j (m t) -> p m j t", t=PACK) for h in range(2)]
-        nc.scalar.copy(w_dst[:, :64], w_src[0])
+        nc.gpsimd.tensor_scalar(w_dst[:, :W_GPSIMD], w_src[0][:, :W_GPSIMD], 1.0, 0.0, ALU.mult, ALU.add)
+        nc.scalar.copy(w_dst[:, W_GPSIMD:64], w_src[0][:, W_GPSIMD:])
         nc.vector.tensor_copy(w_dst[:, 64 : 64 + W_SPLIT], w_src[1][:, :W_SPLIT])
         nc.scalar.copy(w_dst[:, 64 + W_SPLIT :], w_src[1][:, W_SPLIT:])
         w_codes = keep.tile([P, H], U32, name="w_codes", align_bytes=64)
@@ -87,49 +90,68 @@ def tile_picked_selfnormhopnpolar_none_p_kernel(
                 out=w_codes[:, cols].bitcast(FP8X4), scales=w_scales[:, cols], in_=w_bf[:, t * H : (t + 1) * H]
             )
 
-        y_ps = [psum.tile([P, S], F32, name=f"y_ps{t}") for t in range(PACK)]
-        for t in range(PACK):
+        def project(t, a, b, bank):
             cols = slice(t * P, (t + 1) * P)
             nc.tensor.matmul_mx(
-                out=y_ps[t][:], lhsT=w_codes[:, cols].bitcast(FP8X4), lhsT_scale=w_scales[:, cols],
-                rhs=xw[:].bitcast(FP8X4), rhs_scale=xs[:], start=True, stop=True,
+                out=bank[:], lhsT=w_codes[:, cols].bitcast(FP8X4), lhsT_scale=w_scales[:, cols],
+                rhs=xw[:, a:b].bitcast(FP8X4), rhs_scale=xs[:, a:b], start=True, stop=True,
             )
+
+        y0_ps = [psum.tile([P, S // 2], F32, name=name) for name in ("y_ps0", "s_ps3")]
+        project(0, 0, S // 2, y0_ps[0])
+        project(0, S // 2, S, y0_ps[1])
+        y_ps = {t: psum.tile([P, S], F32, name=f"y_ps{t}") for t in range(1, PACK)}
+        for t in range(1, PACK):
+            project(t, 0, S, y_ps[t])
 
         recip = keep.tile([P, 2 * PACK, S], F32, name="recip")
         log1 = [keep.tile([P, 2 * S], F32, name=f"log1_{t}") for t in range(PACK)]
         log2 = [keep.tile([P, S], F32, name=f"log2_{t}") for t in range(PACK)]
-        hop = [keep.tile([P, S], F32, name=f"hop{t}", tag=f"hop{t}") for t in range(PACK)]
+        hop_first = keep.tile([P, S], F32, name="hop_first")
+        hop_last = keep.tile([P, S], F32, name="hop_last", tag="hop3")
+        hop = [hop_first[:], log1[1][:, S:], log1[2][:, S:], hop_last[:]]
+        y_abs = [log1[0][:, S:], y_win[3][:, S : 2 * S], y_win[3][:, 2 * S :], log1[3][:, S:]]
         st = keep.tile([P, PACK, S], F32, name="st")
-        mag = [keep.tile([P, S], F32, name=f"mag{t}") for t in range(PACK - 1)]
-        runs = lambda ap: ap.rearrange("p (a b) -> p a b", b=16)
-        last_mag = recip[:].rearrange("p r (a b) -> p (r a) b", b=P)[:, :, 0:16]
+        gained = keep.tile([P, 2 * PACK, S], F32, name="gained", tag="gained", align_bytes=64)
+        ya = gained[:, :PACK, :]
+        sb = gained[:, PACK:, :]
+        mag_own = [keep.tile([P, S], F32, name=f"mag{t}") for t in range(2)]
+        mag = [
+            mag_own[0][:].rearrange("p (a b) -> p a b", b=32),
+            mag_own[1][:].rearrange("p (a b) -> p a b", b=32),
+            gained[:, 1:, :].rearrange("p r c -> p (r c)").rearrange("p (a b) -> p a b", b=224)[:, :, :32],
+            recip[:].rearrange("p r (a b) -> p (r a) b", b=P)[:, :, :16],
+        ]
 
-        def mag_of(t):
-            return last_mag if t == PACK - 1 else runs(mag[t][:])
+        def like_mag(ap, t):
+            return ap.rearrange("p (a b) -> p a b", b=mag[t].shape[2])
 
         def evac(t):
             nc.scalar.copy(y_win[t][:, :S], y_ps[t][:])
 
+        def evac_vector(t):
+            nc.vector.tensor_copy(y_win[t][:, :S], y_ps[t][:])
+
+        def abs_y_vector(t):
+            nc.vector.scalar_tensor_tensor(y_abs[t], y_ps[t][:], -1.0, y_win[t][:, :S], ALU.mult, ALU.max)
+
         def abs_y(t):
-            nc.scalar.activation(log1[t][:, S:], y_ps[t][:], ACT.Abs)
+            nc.scalar.activation(y_abs[t], y_win[t][:, :S], ACT.Abs)
 
         def log_y(t):
-            nc.scalar.activation(log1[t][:, :S], log1[t][:, S:], ACT.Ln, bias=half[:])
+            nc.scalar.activation(log1[t][:, :S], y_abs[t], ACT.Ln, bias=half[:])
 
         def fetch_hop(t):
-            nc.vector.tensor_copy(hop[t][:], y_win[t][:].indirect(n2_sb[:]))
+            nc.vector.tensor_copy(hop[t], y_win[t][:].indirect(n2_sb[:]))
 
         def step(t):
-            nc.vector.tensor_tensor(st[:, t, :], y_win[t][:, :S], hop[t][:], ALU.subtract)
+            nc.gpsimd.tensor_tensor(st[:, t, :], y_win[t][:, :S], hop[t], ALU.subtract)
 
         def abs_st_vector(t):
-            nc.vector.scalar_tensor_tensor(mag_of(t), runs(st[:, t, :]), -1.0, runs(st[:, t, :]), ALU.mult, ALU.max)
+            nc.vector.scalar_tensor_tensor(mag[t], like_mag(st[:, t, :], t), -1.0, like_mag(st[:, t, :], t), ALU.mult, ALU.max)
 
         def abs_st_scalar(t):
-            nc.scalar.activation(mag_of(t), runs(st[:, t, :]), ACT.Abs)
-
-        ya = keep.tile([P, PACK, S], F32, name="ya")
-        sb = keep.tile([P, PACK, S], F32, name="sb", tag="sb", align_bytes=64)
+            nc.scalar.activation(mag[t], like_mag(st[:, t, :], t), ACT.Abs)
 
         def gain_y(t):
             nc.gpsimd.tensor_scalar(ya[:, t, :], y_win[t][:, :S], ga_sb[:, t : t + 1], 0.0, ALU.mult, ALU.add)
@@ -138,49 +160,56 @@ def tile_picked_selfnormhopnpolar_none_p_kernel(
             nc.gpsimd.tensor_scalar(sb[:, t, :], st[:, t, :], gb_sb[:, t : t + 1], 0.0, ALU.mult, ALU.add)
 
         def log_st(t):
-            nc.scalar.activation(runs(log2[t][:]), mag_of(t), ACT.Ln, bias=half[:])
+            nc.scalar.activation(like_mag(log2[t][:], t), mag[t], ACT.Ln, bias=half[:])
 
-        for t in range(PACK):
+        nc.scalar.copy(y_win[0][:, : S // 2], y0_ps[0][:])
+        nc.vector.tensor_copy(y_win[0][:, S // 2 : S], y0_ps[1][:])
+        for t in range(1, PACK):
             evac(t)
-            gain_y(t)
-        fetch_hop(0)
-        fetch_hop(1)
+        gain_y(0)
+        for t in range(PACK):
+            fetch_hop(t)
+            step(t)
         abs_y(0)
-        abs_y(1)
-        step(0)
-        step(1)
         log_y(0)
-        log_y(1)
-        abs_st_vector(0)
-        fetch_hop(2)
-        abs_st_vector(1)
-        fetch_hop(3)
-        abs_y(2)
-        abs_y(3)
-        log_st(0)
-        log_y(2)
-        log_st(1)
-        log_y(3)
-        step(2)
-        step(3)
-        abs_st_scalar(2)
-        abs_st_vector(3)
-        log_st(2)
-        log_st(3)
+        for t in range(1, PACK):
+            abs_y_vector(t)
+        for t in range(2):
+            abs_st_scalar(t)
+            log_st(t)
+        for t in range(1, PACK):
+            log_y(t)
+        for t in range(2, PACK):
+            abs_st_vector(t)
+        for t in range(2, PACK):
+            log_st(t)
+        for t in range(1, PACK):
+            gain_y(t)
         for t in range(PACK):
             gain_st(t)
 
         fetched = keep.tile([P, PACK, S], F32, name="fetched", tag=f"hop{PACK - 1}")
         for t in range(PACK):
             nc.vector.tensor_copy(fetched[:, t, :], log1[t][:].indirect(n1_sb[:]))
-        for t in range(PACK):
+
+        def recip_y(t):
             nc.scalar.activation(recip[:, t, :], fetched[:, t, :], ACT.Exp, scale=-1.0)
+
+        def recip_st(t, a, b):
+            nc.scalar.activation(
+                recip[:, PACK + t, a:b], log2[t][:].indirect(n3_sb[:, a // 16 : b // 16]), ACT.Exp, scale=-1.0
+            )
+
+        for t in range(PACK - 1):
+            recip_y(t)
+        recip_st(0, *CHUNKS[0])
+        recip_y(PACK - 1)
 
         z_bf = keep.tile([P, PACK * S], BF16, name="z_bf", align_bytes=64)
         dealt = "p t (m u) -> p m t u"
         nc.vector.tensor_tensor(
             z_bf[:].rearrange("p (u m t) -> p m t u", u=PACK, t=PACK),
-            ya[:].rearrange(dealt, u=PACK), recip[:, :PACK, :].rearrange(dealt, u=PACK), ALU.mult,
+            ya.rearrange(dealt, u=PACK), recip[:, :PACK, :].rearrange(dealt, u=PACK), ALU.mult,
         )
         z_first = keep.tile([P, P], U32, name="z_first", align_bytes=64)
         z_scales = keep.tile([P, S], U8, name="z_scales", align_bytes=64)
@@ -191,10 +220,8 @@ def tile_picked_selfnormhopnpolar_none_p_kernel(
         z2_scales = keep.tile([P, S], U8, name="z2_scales", align_bytes=64)
         woven = "p t (c i) -> p c t i"
         for a, b in CHUNKS:
-            for t in range(PACK):
-                nc.scalar.activation(
-                    recip[:, PACK + t, a:b], log2[t][:].indirect(n3_sb[:, a // 16 : b // 16]), ACT.Exp, scale=-1.0
-                )
+            for t in range(1 if a == 0 else 0, PACK):
+                recip_st(t, a, b)
             nc.vector.tensor_tensor(
                 z2_bf[:, PACK * a : PACK * b].rearrange("p (c i t) -> p c t i", i=4, t=PACK),
                 sb[:, :, a:b].rearrange(woven, i=4), recip[:, PACK:, a:b].rearrange(woven, i=4), ALU.mult,
@@ -203,7 +230,7 @@ def tile_picked_selfnormhopnpolar_none_p_kernel(
                 out=z2_codes[:, a:b].bitcast(FP8X4), scales=z2_scales[:, a:b], in_=z2_bf[:, PACK * a : PACK * b]
             )
 
-        z_rest = keep.tile([P, S - P], U32, name="z_rest", tag="sb", align_bytes=64)
+        z_rest = keep.tile([P, S - P], U32, name="z_rest", tag="gained", align_bytes=64)
         for a, b in [(1, 2), (2, 4)]:
             nc.vector.quantize_mx(
                 out=z_rest[:, (a - 1) * P : (b - 1) * P].bitcast(FP8X4), scales=z_scales[:, a * P : b * P], in_=z_bf[:, a * S : b * S]

@@ -19,8 +19,8 @@ P = 128
 PACK = 4
 VECTOR_FETCHED = 4
 CHUNKS = [(0, 256), (256, 384), (384, 512)]
-W_SPLIT = 40
-W_GPSIMD = 24
+W_SPLIT = 46
+W_PIECES = [(0, 256), (256, 512)]
 
 
 def tile_picked_selfnormhopnpolar_none_p_kernel(
@@ -48,9 +48,9 @@ def tile_picked_selfnormhopnpolar_none_p_kernel(
         x_table = keep.tile([P, T], I32, name="x_table", align_bytes=64)
         nc.sync.dma_start(x_table[:], x_words[0].rearrange("p n t -> p (n t)").bitcast(I32))
         w_rows = w1.rearrange("(p j) c -> p j c", j=PACK)
-        w_raw = [keep.tile([P, PACK, H // 2], F32, name=f"w_raw{h}") for h in range(2)]
-        for h in range(2):
-            nc.sync.dma_start(w_raw[h][:], w_rows[:, :, h * (H // 2) : (h + 1) * (H // 2)])
+        w_raw = [keep.tile([P, PACK, b - a], F32, name=f"w_raw{a}") for a, b in W_PIECES]
+        for piece, (a, b) in zip(w_raw, W_PIECES):
+            nc.sync.dma_start(piece[:], w_rows[:, :, a:b])
         n3_sb = load_list(n3, "n3_sb")
         n4_sb = load_list(n4, "n4_sb")
         n5_sb = load_list(n5, "n5_sb")
@@ -78,10 +78,10 @@ def tile_picked_selfnormhopnpolar_none_p_kernel(
         w_bf = keep.tile([P, PACK * H], BF16, name="w_bf", align_bytes=64)
         w_dst = w_bf[:].rearrange("p (t m j) -> p m j t", t=PACK, j=PACK)
         w_src = [w_raw[h][:].rearrange("p j (m t) -> p m j t", t=PACK) for h in range(2)]
-        nc.gpsimd.tensor_scalar(w_dst[:, :W_GPSIMD], w_src[0][:, :W_GPSIMD], 1.0, 0.0, ALU.mult, ALU.add)
-        nc.scalar.copy(w_dst[:, W_GPSIMD:64], w_src[0][:, W_GPSIMD:])
-        nc.vector.tensor_copy(w_dst[:, 64 : 64 + W_SPLIT], w_src[1][:, :W_SPLIT])
-        nc.scalar.copy(w_dst[:, 64 + W_SPLIT :], w_src[1][:, W_SPLIT:])
+        m1 = W_PIECES[0][1] // PACK
+        nc.scalar.copy(w_dst[:, :m1], w_src[0])
+        nc.vector.tensor_copy(w_dst[:, m1 : m1 + W_SPLIT], w_src[1][:, :W_SPLIT])
+        nc.scalar.copy(w_dst[:, m1 + W_SPLIT :], w_src[1][:, W_SPLIT:])
         w_codes = keep.tile([P, H], U32, name="w_codes", align_bytes=64)
         w_scales = keep.tile([P, H], U8, name="w_scales", align_bytes=64)
         for t in range(PACK):
@@ -185,12 +185,15 @@ def tile_picked_selfnormhopnpolar_none_p_kernel(
             log_st(t)
         for t in range(1, PACK):
             gain_y(t)
-        for t in range(PACK):
+        for t in range(2):
             gain_st(t)
 
         fetched = keep.tile([P, PACK, S], F32, name="fetched", tag=f"hop{PACK - 1}")
         for t in range(PACK):
             nc.vector.tensor_copy(fetched[:, t, :], log1[t][:].indirect(n1_sb[:]))
+
+        for t in range(2, PACK):
+            nc.vector.tensor_scalar_mul(sb[:, t, :], st[:, t, :], gb_sb[:, t : t + 1])
 
         def recip_y(t):
             nc.scalar.activation(recip[:, t, :], fetched[:, t, :], ACT.Exp, scale=-1.0)
@@ -260,16 +263,18 @@ def tile_picked_selfnormhopnpolar_none_p_kernel(
         sq = [keep.tile([P, 2, W], F32, name=f"sq{u}") for u in range(PACK)]
         ssum = [keep.tile([P, W], F32, name=f"ssum{u}") for u in range(PACK)]
         ra = [keep.tile([P, W], F32, name=f"ra{u}") for u in range(PACK)]
+        rb = [keep.tile([P, W], F32, name=f"rb{u}") for u in range(PACK)]
         res = [keep.tile([P, S], F32, name=f"res{u}") for u in range(PACK)]
 
         def fetch(u):
             nc.vector.tensor_scalar(pa[u][:], s_win[u][:].indirect(n4_sb[:]), -0.5, 0.0, ALU.mult, ALU.add)
             nc.vector.tensor_copy(pb[u][:], s_win[u][:].indirect(n5_sb[:]))
+            nc.gpsimd.tensor_tensor(rb[u][:], pb[u][:], pa[u][:], ALU.add)
             nc.scalar.activation(sq[u][:, 0, :], pa[u][:], ACT.Square, scale=2.0)
             nc.scalar.activation(sq[u][:, 1, :], pb[u][:], ACT.Square)
 
         def put_rb(u):
-            nc.vector.tensor_tensor(res[u][:].indirect(n5_sb[:]), pb[u][:], pa[u][:], ALU.add)
+            nc.vector.tensor_copy(res[u][:].indirect(n5_sb[:]), rb[u][:])
 
         def radius(u):
             nc.gpsimd.tensor_tensor(ssum[u][:], sq[u][:, 0, :], sq[u][:, 1, :], ALU.add)

from contextlib import ExitStack

import concourse.mybir as mybir

K, T, S, H, W = 512, 2048, 512, 512, 256
FLOPS = 2 * K * H * S + 2 * H * S * S

F32 = mybir.dt.float32
BF16 = mybir.dt.bfloat16
I32 = mybir.dt.int32
U32 = mybir.dt.uint32
U16 = mybir.dt.uint16
U8 = mybir.dt.uint8
FP8X4 = mybir.dt.float8_e4m3fn_x4
ACT = mybir.ActivationFunctionType
ALU = mybir.AluOpType

P = 128
PACK = 4
VECTOR_FETCHED = 4
CHUNKS = [(0, 256), (256, 384), (384, 512)]
W_SPLIT = 46
W_PIECES = [(0, 256), (256, 512)]


def tile_picked_selfnormhopnpolar_none_p_kernel(
    tc, x_words, x_scales, w1, ga, gb, offs, n1, n2, n3, n4, n5, out
):
    nc = tc.nc
    with ExitStack() as ctx:
        keep = ctx.enter_context(tc.tile_pool(name="keep", bufs=1))
        psum = ctx.enter_context(tc.psum_pool(name="psum", bufs=1))

        def load_list(src, name):
            t = keep.tile([P, src.shape[1]], U16, name=name)
            nc.sync.dma_start(t[:], src)
            return t

        x_bytes = keep.tile([P, T], U8, name="x_bytes", align_bytes=64)
        nc.gpsimd.memset(x_bytes[:, : T // 2].bitcast(I32), 0)
        nc.vector.memset(x_bytes[:, T // 2 :].bitcast(I32), 0)
        for q in range(4):
            nc.scalar.dma_start(x_bytes[32 * q : 32 * q + 4, :].bitcast(I32), x_scales[0, 4 * q : 4 * q + 4, :].bitcast(I32))

        offs_sb = load_list(offs, "offs_sb")
        n2_sb = load_list(n2, "n2_sb")
        n1_sb = load_list(n1, "n1_sb")
        x_table = keep.tile([P, T], I32, name="x_table", align_bytes=64)
        nc.sync.dma_start(x_table[:], x_words[0].rearrange("p n t -> p (n t)").bitcast(I32))
        w_rows = w1.rearrange("(p j) c -> p j c", j=PACK)
        w_raw = [keep.tile([P, PACK, b - a], F32, name=f"w_raw{a}") for a, b in W_PIECES]
        for piece, (a, b) in zip(w_raw, W_PIECES):
            nc.sync.dma_start(piece[:], w_rows[:, :, a:b])
        n3_sb = load_list(n3, "n3_sb")
        n4_sb = load_list(n4, "n4_sb")
        n5_sb = load_list(n5, "n5_sb")
        ga_sb = keep.tile([P, PACK], F32, name="ga_sb")
        nc.sync.dma_start(ga_sb[:], ga.rearrange("(p t) o -> p (t o)", t=PACK))
        gb_sb = keep.tile([P, PACK], F32, name="gb_sb")
        nc.sync.dma_start(gb_sb[:], gb.rearrange("(p t) o -> p (t o)", t=PACK))

        y_win = [keep.tile([P, (3 if t == PACK - 1 else 2) * S], F32, name=f"y_win{t}") for t in range(PACK)]
        nc.gpsimd.memset(y_win[0][:, S:], 0.0)
        half = keep.tile([P, 1], F32, name="half")
        nc.gpsimd.memset(half[:], 0.5)
        quarter = keep.tile([P, 1], F32, name="quarter")
        nc.gpsimd.memset(quarter[:], 0.25)
        warm = keep.tile([P, 1], F32, name="warm")
        nc.scalar.activation(warm[:], half[:], ACT.Ln, bias=half[:])
        for t in range(1, PACK):
            nc.vector.memset(y_win[t][:, S:], 0.0)

        xw = keep.tile([P, S], U32, name="xw", align_bytes=64)
        nc.vector.tensor_copy(xw[:], x_table[:].bitcast(U32).indirect(offs_sb[:]))
        xs = keep.tile([P, S], U8, name="xs", align_bytes=64)
        nc.vector.tensor_copy(xs[:], x_bytes[:].indirect(offs_sb[:]))

        w_bf = keep.tile([P, PACK * H], BF16, name="w_bf", align_bytes=64)
        w_dst = w_bf[:].rearrange("p (t m j) -> p m j t", t=PACK, j=PACK)
        w_src = [w_raw[h][:].rearrange("p j (m t) -> p m j t", t=PACK) for h in range(2)]
        m1 = W_PIECES[0][1] // PACK
        nc.scalar.copy(w_dst[:, :m1], w_src[0])
        nc.vector.tensor_copy(w_dst[:, m1 : m1 + W_SPLIT], w_src[1][:, :W_SPLIT])
        nc.scalar.copy(w_dst[:, m1 + W_SPLIT :], w_src[1][:, W_SPLIT:])
        w_codes = keep.tile([P, H], U32, name="w_codes", align_bytes=64)
        w_scales = keep.tile([P, H], U8, name="w_scales", align_bytes=64)
        for t in range(PACK):
            cols = slice(t * P, (t + 1) * P)
            nc.vector.quantize_mx(
                out=w_codes[:, cols].bitcast(FP8X4), scales=w_scales[:, cols], in_=w_bf[:, t * H : (t + 1) * H]
            )

        def project(t, a, b, bank):
            cols = slice(t * P, (t + 1) * P)
            nc.tensor.matmul_mx(
                out=bank[:], lhsT=w_codes[:, cols].bitcast(FP8X4), lhsT_scale=w_scales[:, cols],
                rhs=xw[:, a:b].bitcast(FP8X4), rhs_scale=xs[:, a:b], start=True, stop=True,
            )

        y0_ps = [psum.tile([P, S // 2], F32, name=name) for name in ("y_ps0", "s_ps3")]
        project(0, 0, S // 2, y0_ps[0])
        project(0, S // 2, S, y0_ps[1])
        y_ps = {t: psum.tile([P, S], F32, name=f"y_ps{t}") for t in range(1, PACK)}
        for t in range(1, PACK):
            project(t, 0, S, y_ps[t])

        recip = keep.tile([P, 2 * PACK, S], F32, name="recip")
        log1 = [keep.tile([P, 2 * S], F32, name=f"log1_{t}") for t in range(PACK)]
        log2 = [keep.tile([P, S], F32, name=f"log2_{t}") for t in range(PACK)]
        hop_first = keep.tile([P, S], F32, name="hop_first")
        hop_last = keep.tile([P, S], F32, name="hop_last", tag="hop3")
        hop = [hop_first[:], log1[1][:, S:], log1[2][:, S:], hop_last[:]]
        y_abs = [log1[0][:, S:], y_win[3][:, S : 2 * S], y_win[3][:, 2 * S :], log1[3][:, S:]]
        st = keep.tile([P, PACK, S], F32, name="st")
        gained = keep.tile([P, 2 * PACK, S], F32, name="gained", tag="gained", align_bytes=64)
        ya = gained[:, :PACK, :]
        sb = gained[:, PACK:, :]
        mag_own = [keep.tile([P, S], F32, name=f"mag{t}") for t in range(2)]
        mag = [
            mag_own[0][:].rearrange("p (a b) -> p a b", b=32),
            mag_own[1][:].rearrange("p (a b) -> p a b", b=32),
            gained[:, 1:, :].rearrange("p r c -> p (r c)").rearrange("p (a b) -> p a b", b=224)[:, :, :32],
            recip[:].rearrange("p r (a b) -> p (r a) b", b=P)[:, :, :16],
        ]

        def like_mag(ap, t):
            return ap.rearrange("p (a b) -> p a b", b=mag[t].shape[2])

        def evac(t):
            nc.scalar.copy(y_win[t][:, :S], y_ps[t][:])

        def evac_vector(t):
            nc.vector.tensor_copy(y_win[t][:, :S], y_ps[t][:])

        def abs_y_vector(t):
            nc.vector.scalar_tensor_tensor(y_abs[t], y_ps[t][:], -1.0, y_win[t][:, :S], ALU.mult, ALU.max)

        def abs_y(t):
            nc.scalar.activation(y_abs[t], y_win[t][:, :S], ACT.Abs)

        def log_y(t):
            nc.scalar.activation(log1[t][:, :S], y_abs[t], ACT.Ln, bias=half[:])

        def fetch_hop(t):
            nc.vector.tensor_copy(hop[t], y_win[t][:].indirect(n2_sb[:]))

        def step(t):
            nc.gpsimd.tensor_tensor(st[:, t, :], y_win[t][:, :S], hop[t], ALU.subtract)

        def abs_st_vector(t):
            nc.vector.scalar_tensor_tensor(mag[t], like_mag(st[:, t, :], t), -1.0, like_mag(st[:, t, :], t), ALU.mult, ALU.max)

        def abs_st_scalar(t):
            nc.scalar.activation(mag[t], like_mag(st[:, t, :], t), ACT.Abs)

        def gain_y(t):
            nc.gpsimd.tensor_scalar(ya[:, t, :], y_win[t][:, :S], ga_sb[:, t : t + 1], 0.0, ALU.mult, ALU.add)

        def gain_st(t):
            nc.gpsimd.tensor_scalar(sb[:, t, :], st[:, t, :], gb_sb[:, t : t + 1], 0.0, ALU.mult, ALU.add)

        def log_st(t):
            nc.scalar.activation(like_mag(log2[t][:], t), mag[t], ACT.Ln, bias=half[:])

        nc.scalar.copy(y_win[0][:, : S // 2], y0_ps[0][:])
        nc.vector.tensor_copy(y_win[0][:, S // 2 : S], y0_ps[1][:])
        for t in range(1, PACK):
            evac(t)
        gain_y(0)
        for t in range(PACK):
            fetch_hop(t)
            step(t)
        abs_y(0)
        log_y(0)
        for t in range(1, PACK):
            abs_y_vector(t)
        for t in range(2):
            abs_st_scalar(t)
            log_st(t)
        for t in range(1, PACK):
            log_y(t)
        for t in range(2, PACK):
            abs_st_vector(t)
        for t in range(2, PACK):
            log_st(t)
        for t in range(1, PACK):
            gain_y(t)
        for t in range(2):
            gain_st(t)

        fetched = keep.tile([P, PACK, S], F32, name="fetched", tag=f"hop{PACK - 1}")
        for t in range(PACK):
            nc.vector.tensor_copy(fetched[:, t, :], log1[t][:].indirect(n1_sb[:]))

        for t in range(2, PACK):
            nc.vector.tensor_scalar_mul(sb[:, t, :], st[:, t, :], gb_sb[:, t : t + 1])

        def recip_y(t):
            nc.scalar.activation(recip[:, t, :], fetched[:, t, :], ACT.Exp, scale=-1.0)

        def recip_st(t, a, b):
            nc.scalar.activation(
                recip[:, PACK + t, a:b], log2[t][:].indirect(n3_sb[:, a // 16 : b // 16]), ACT.Exp, scale=-1.0
            )

        for t in range(PACK - 1):
            recip_y(t)
        recip_st(0, *CHUNKS[0])
        recip_y(PACK - 1)

        z_bf = keep.tile([P, PACK * S], BF16, name="z_bf", align_bytes=64)
        dealt = "p t (m u) -> p m t u"
        nc.vector.tensor_tensor(
            z_bf[:].rearrange("p (u m t) -> p m t u", u=PACK, t=PACK),
            ya.rearrange(dealt, u=PACK), recip[:, :PACK, :].rearrange(dealt, u=PACK), ALU.mult,
        )
        z_first = keep.tile([P, P], U32, name="z_first", align_bytes=64)
        z_scales = keep.tile([P, S], U8, name="z_scales", align_bytes=64)
        nc.vector.quantize_mx(out=z_first[:].bitcast(FP8X4), scales=z_scales[:, :P], in_=z_bf[:, :S])

        z2_bf = keep.tile([P, PACK * S], BF16, name="z2_bf", align_bytes=64)
        z2_codes = keep.tile([P, S], U32, name="z2_codes", align_bytes=64)
        z2_scales = keep.tile([P, S], U8, name="z2_scales", align_bytes=64)
        woven = "p t (c i) -> p c t i"
        for a, b in CHUNKS:
            for t in range(1 if a == 0 else 0, PACK):
                recip_st(t, a, b)
            nc.vector.tensor_tensor(
                z2_bf[:, PACK * a : PACK * b].rearrange("p (c i t) -> p c t i", i=4, t=PACK),
                sb[:, :, a:b].rearrange(woven, i=4), recip[:, PACK:, a:b].rearrange(woven, i=4), ALU.mult,
            )
            nc.vector.quantize_mx(
                out=z2_codes[:, a:b].bitcast(FP8X4), scales=z2_scales[:, a:b], in_=z2_bf[:, PACK * a : PACK * b]
            )

        z_rest = keep.tile([P, S - P], U32, name="z_rest", tag="gained", align_bytes=64)
        for a, b in [(1, 2), (2, 4)]:
            nc.vector.quantize_mx(
                out=z_rest[:, (a - 1) * P : (b - 1) * P].bitcast(FP8X4), scales=z_scales[:, a * P : b * P], in_=z_bf[:, a * S : b * S]
            )
        z_codes = [z_first[:]] + [z_rest[:, u * P : (u + 1) * P] for u in range(PACK - 1)]
        s_win = [keep.tile([P, S], F32, name=f"s_win{u}") for u in range(PACK)]

        def product(u, pieces, bank):
            cols = slice(u * P, (u + 1) * P)
            for a, b in pieces:
                nc.tensor.matmul_mx(
                    out=bank[:, a:b], lhsT=z_codes[u].bitcast(FP8X4), lhsT_scale=z_scales[:, cols],
                    rhs=z2_codes[:, a:b].bitcast(FP8X4), rhs_scale=z2_scales[:, a:b], start=True, stop=True,
                )
            a, b = pieces[0][0], pieces[-1][1]
            nc.scalar.activation(s_win[u][:, a:b], bank[:, a:b], ACT.Copy, scale=0.0625)

        s_early = psum.tile([P, S], F32, name="y_ps0")
        product(0, CHUNKS[:-1], s_early)
        for u in range(PACK):
            s_ps = psum.tile([P, S], F32, name=f"s_ps{u}")
            product(u, CHUNKS[-1:] if u == 0 else [(0, S)], s_ps)

        out_rows = out.rearrange("(m u) j -> u m j", u=PACK)
        pa = [keep.tile([P, W], F32, name=f"pa{u}") for u in range(PACK)]
        pb = [keep.tile([P, W], F32, name=f"pb{u}") for u in range(PACK)]
        sq = [keep.tile([P, 2, W], F32, name=f"sq{u}") for u in range(PACK)]
        ssum = [keep.tile([P, W], F32, name=f"ssum{u}") for u in range(PACK)]
        ra = [keep.tile([P, W], F32, name=f"ra{u}") for u in range(PACK)]
        rb = [keep.tile([P, W], F32, name=f"rb{u}") for u in range(PACK)]
        res = [keep.tile([P, S], F32, name=f"res{u}") for u in range(PACK)]

        def fetch(u):
            nc.vector.tensor_scalar(pa[u][:], s_win[u][:].indirect(n4_sb[:]), -0.5, 0.0, ALU.mult, ALU.add)
            nc.vector.tensor_copy(pb[u][:], s_win[u][:].indirect(n5_sb[:]))
            nc.gpsimd.tensor_tensor(rb[u][:], pb[u][:], pa[u][:], ALU.add)
            nc.scalar.activation(sq[u][:, 0, :], pa[u][:], ACT.Square, scale=2.0)
            nc.scalar.activation(sq[u][:, 1, :], pb[u][:], ACT.Square)

        def put_rb(u):
            nc.vector.tensor_copy(res[u][:].indirect(n5_sb[:]), rb[u][:])

        def radius(u):
            nc.gpsimd.tensor_tensor(ssum[u][:], sq[u][:, 0, :], sq[u][:, 1, :], ALU.add)
            nc.scalar.activation(ra[u][:], ssum[u][:], ACT.Sqrt, bias=quarter[:])

        def put_ra(u):
            nc.vector.tensor_copy(res[u][:].indirect(n4_sb[:]), ra[u][:])
            nc.sync.dma_start(out_rows[u], res[u][:])

        fetch(0)
        for u in range(PACK):
            if u + 1 < PACK:
                fetch(u + 1)
            radius(u)
            put_rb(u)
            put_ra(u)
